import numpy as np
import ml_dtypes


def mxq(x, axis, fmt="e4m3"):
    dtype, down = {"e4m3": (ml_dtypes.float8_e4m3fn, 7), "e5m2": (ml_dtypes.float8_e5m2, 14)}[fmt]
    v = np.moveaxis(np.asarray(x, np.float32).astype(ml_dtypes.bfloat16).astype(np.float64), axis, -1)
    blocks = v.reshape(v.shape[:-1] + (-1, 32))
    amax = np.abs(blocks).max(-1, keepdims=True)
    byte = np.maximum(np.where(amax > 0, np.frexp(amax)[1] - 1 + 127, 0) - down, 1)
    scale = np.exp2(byte - 127.0)
    codes = (blocks / scale).astype(np.float32).astype(dtype).astype(np.float64)
    return np.moveaxis((codes * scale).reshape(v.shape), -1, axis)


WIDE = False


def mx_kscale(k):
    if not WIDE:
        return np.ones(k)
    levels = np.array([10, -10, 5, -5, 0])
    if k % 512:
        return np.exp2(np.random.permutation(np.resize(levels, k // 32))).repeat(32)
    a = np.empty((k // 512, 16))
    for p in range(k // 512):
        a[p, :8] = np.random.permutation(np.resize(levels, 8))
        for g in range(8):
            far = levels[np.abs(levels - a[p, g]) >= 10]
            a[p, g + 8] = far[np.random.randint(len(far))]
    return np.exp2(a.ravel()).repeat(32)


def f64(x):
    return np.asarray(x).astype(np.float64)


def striped(idx):
    return np.tile(idx.reshape(-1, 16).T, (8, 1)).astype(np.uint16)


def unstriped(offs):
    return offs[:16].T.reshape(-1).astype(np.int64)


E2M1 = np.array([0.0, 0.5, 1.0, 1.5, 2.0, 3.0, 4.0, 6.0, -0.0, -0.5, -1.0, -1.5, -2.0, -3.0, -4.0, -6.0])


def pack_weight(w, fmt):
    k, n = w.shape
    w = f64(np.asarray(w, np.float32).astype(ml_dtypes.bfloat16)).reshape(k // 32, 32, n)
    amax = np.abs(w).max(1)
    if fmt == "e4m3":
        byte = np.frexp(amax)[1] - 1 + 127 - 7
    else:
        mant, ex = np.frexp(amax / 6.0)
        byte = np.where(mant > 0.5, ex, ex - 1) + 127
    byte = np.clip(np.where(amax > 0, byte, 1), 1, 254)
    scaled = (w * np.exp2(127.0 - byte)[:, None, :]).reshape(k, n).astype(np.float32)
    by_word = np.ascontiguousarray(scaled.reshape(k // 512, 128, 4, n).transpose(0, 1, 3, 2))
    if fmt == "e4m3":
        words = by_word.astype(ml_dtypes.float8_e4m3fn).view(np.uint8)
    else:
        c = by_word.astype(ml_dtypes.float4_e2m1fn).view(np.uint8) & 0xF
        words = (c[..., 0::2] | (c[..., 1::2] << 4)).reshape(k // 512, 128, 2 * n)
    return np.ascontiguousarray(words), np.ascontiguousarray(byte.astype(np.uint8).reshape(k // 512, 16, n))


def unpack_weight(words, scales, fmt):
    g, _, n = scales.shape
    words = np.ascontiguousarray(words).reshape(g, 128, n, -1)
    if fmt == "e4m3":
        vals = words.view(ml_dtypes.float8_e4m3fn).astype(np.float64)
    else:
        nib = np.empty((g, 128, n, 4), np.uint8)
        nib[..., 0::2] = words & 0xF
        nib[..., 1::2] = words >> 4
        vals = E2M1[nib]
    vals = vals * np.repeat(np.exp2(scales.astype(np.float64) - 127.0), 8, axis=1)[..., None]
    return vals.transpose(0, 1, 3, 2).reshape(g * 512, n)


def gelu(v):
    return 0.5 * v * (1.0 + np.tanh(np.sqrt(2.0 / np.pi) * (v + 0.044715 * v**3)))


K, T, S, H, T2, P, N = 1536, 4096, 1024, 512, 2048, 1024, 512

def setup_inputs():
    n = np.random.standard_normal
    s = mx_kscale(K)[:, None]
    u = mx_kscale(H)[:, None]
    d = {}
    d["tab_words"], d["tab_scales"] = pack_weight(n((K, T)) * s, "e4m3")
    d["offs"] = striped(np.random.permutation(T)[:S])
    d["w1"] = (n((K, H)) / K ** 0.5 / s).astype(np.float32)
    d["cap"] = (0.3 + 0.8 * n((H, S))).astype(np.float32)
    d["gain"] = (np.exp(0.3 * n(H)) * u[:, 0]).astype(np.float32)
    d["page0"] = (0.8 * n((H, T2)) * u).astype(np.float32)
    d["wgs"] = np.exp(0.3 * n((128, S))).astype(np.float32)
    d["offs2"] = striped(np.random.permutation(T2)[:S])
    d["offs3"] = striped(np.random.permutation(T2)[:P])
    d["base"] = (0.5 * n(H) * u[:, 0]).astype(np.float32)
    d["w2_words"], d["w2_scales"] = pack_weight(1.5 * n((H, N)) / H ** 0.5 / u, "e2m1")
    d["w3"] = (n((H, N)) / H ** 0.5 / u).astype(np.float32)
    d["keep"] = (0.8 * np.exp(0.3 * n(H)) / u[:, 0]).astype(np.float32)
    d["page1"] = n((N, T2)).astype(np.float32)
    d["wgo"] = np.exp(0.3 * n((128, P))).astype(np.float32)
    d["offs4"] = striped(np.random.permutation(T2)[:P])
    return d

def reference(tab_words, tab_scales, offs, w1, cap, gain, page0, wgs, offs2, offs3, base, w2_words, w2_scales, w3, keep, page1, wgo, offs4):
    v = unpack_weight(tab_words, tab_scales, "e4m3")[:, unstriped(offs)]
    h = f64(gain)[:, None] * np.minimum(mxq(f64(w1), 0, "e4m3").T @ v, f64(cap))
    page = f64(page0).copy()
    page[:, unstriped(offs2)] = np.tile(f64(wgs), (H // 128, 1)) * h
    x = page[:, unstriped(offs3)] + f64(base)[:, None]
    xq = mxq(x, 0, "e4m3")
    bounded = np.tanh(unpack_weight(w2_words, w2_scales, "e2m1").T @ xq)
    other = (mxq(f64(w3), 0, "e4m3").T @ xq) - f64(keep)[:, None] * x
    y = bounded + other
    out = f64(page1).copy()
    out[:, unstriped(offs4)] = np.tile(f64(wgo), (N // 128, 1)) * y
    return out

@@ -1,0 +1,335 @@
+from contextlib import ExitStack
+
+import concourse.mybir as mybir
+from concourse.masks import make_identity
+
+K, T, S, H, T2, P, N = 1536, 4096, 1024, 512, 2048, 1024, 512
+FLOPS = 2 * K * H * S + 2 * 2 * H * N * P
+
+F32 = mybir.dt.float32
+BF16 = mybir.dt.bfloat16
+I32 = mybir.dt.int32
+U32 = mybir.dt.uint32
+U16 = mybir.dt.uint16
+U8 = mybir.dt.uint8
+FP8X4 = mybir.dt.float8_e4m3fn_x4
+FP4X4 = mybir.dt.float4_e2m1fn_x4
+ALU = mybir.AluOpType
+ACT = mybir.ActivationFunctionType
+
+PART = 128
+PASSES = K // 512
+SLABS = H // PART
+HALF = S // 2
+CHUNK = 256
+CHUNKS = P // CHUNK
+
+
+def tile_list_cork_batch_page_kernel(
+    tc, tab_words, tab_scales, offs, w1, cap, gain, page0, wgs, offs2, offs3, base,
+    w2_words, w2_scales, w3, keep, page1, wgo, offs4, out,
+):
+    nc = tc.nc
+    with ExitStack() as ctx:
+        lists = ctx.enter_context(tc.tile_pool(name="lists", bufs=1))
+        sb = ctx.enter_context(tc.tile_pool(name="sb", bufs=1))
+        psum = ctx.enter_context(tc.psum_pool(name="psum", bufs=1))
+
+        def load_list(src, name):
+            t = lists.tile([PART, S // 16], U16, name=name)
+            nc.sync.dma_start(t[:], src)
+            return t
+
+        def entries(list_tile, first, count):
+            return list_tile[:, first // 16 : (first + count) // 16]
+
+        warm = sb.tile([PART, 8], F32, name="warm")
+        nc.vector.memset(warm[:, 0:1], 0.0)
+        nc.scalar.activation(warm[:, 4:5], warm[:, 0:1], ACT.Tanh)
+
+        ident = sb.tile([PART, PART], F32, name="ident")
+        make_identity(nc, ident[:])
+        tab_sc = sb.tile([PART, T], U8, name="tab_sc", tag="tab_sc", align_bytes=64)
+        nc.vector.memset(tab_sc[:].bitcast(I32), 0)
+        for q in range(4):
+            nc.gpsimd.dma_start(
+                tab_sc[32 * q : 32 * q + 4 * PASSES, :].bitcast(I32),
+                tab_scales[:, 4 * q : 4 * q + 4, :].bitcast(I32),
+            )
+        w2_sc = sb.tile([PART, N], U8, name="w2_sc", align_bytes=64)
+        nc.vector.memset(w2_sc[:].bitcast(I32), 0)
+
+        def load_vector(vec, name):
+            t = sb.tile([PART, SLABS], F32, name=name)
+            with nc.allow_non_contiguous_dma(reason="one value for each partition and slab"):
+                nc.sync.dma_start(t[:], vec.rearrange("(s p) -> p s", p=PART))
+            return t
+
+        def interleave(copy, dst, src):
+            copy(
+                dst.rearrange("p (c k i) -> p c i k", k=4, i=4),
+                src.rearrange("p i (c k) -> p c i k", k=4),
+            )
+
+        def load_w1(s):
+            raws = []
+            for a in range(PASSES):
+                raw = sb.tile([PART, 4, PART], F32, name="w1_raw", tag="w1_raw", bufs=2 * PASSES)
+                nc.sync.dma_start(
+                    raw[:],
+                    w1[512 * a : 512 * (a + 1), PART * s : PART * (s + 1)].rearrange("(p i) c -> p i c", i=4),
+                )
+                raws.append(raw)
+            return raws
+
+        def quantise_w1(s, raws):
+            copy = nc.vector.tensor_copy if s == 0 else nc.scalar.copy
+            codes = sb.tile([PART, PASSES * PART], U32, name="w1_codes%d" % s, align_bytes=64)
+            scales = sb.tile([PART, PASSES * PART], U8, name="w1_scales%d" % s, align_bytes=64)
+            for lo, hi, tag in ((0, 2, "w1_bf%d" % s), (2, 3, "w1_bf_last")):
+                grouped = sb.tile([PART, 512 * (hi - lo)], BF16, name="w1_bf", tag=tag, align_bytes=64)
+                for a in range(lo, hi):
+                    interleave(copy, grouped[:, 512 * (a - lo) : 512 * (a - lo + 1)], raws[a][:])
+                nc.vector.quantize_mx(
+                    codes[:, PART * lo : PART * hi].bitcast(FP8X4), scales[:, PART * lo : PART * hi], grouped[:]
+                )
+            return codes, scales
+
+        idx = load_list(offs, "idx")
+        w1_raw = {0: load_w1(0)}
+        tab_w = []
+        for a in range(PASSES):
+            t = sb.tile([PART, T], U32, name="tab_w", tag="big%d" % a, align_bytes=64)
+            nc.sync.dma_start(t[:].bitcast(I32), tab_words[a].rearrange("p t i -> p (t i)").bitcast(I32))
+            tab_w.append(t)
+        gain_sb = load_vector(gain, "gain_sb")
+        wgs_sb = sb.tile([PART, S], F32, name="wgs_sb")
+        cap_sb = [sb.tile([PART, S], F32, name="cap_sb%d" % s) for s in range(SLABS)]
+        page0_sb = [sb.tile([PART, T2], F32, name="page0_sb%d" % s) for s in range(SLABS)]
+
+        def rows(s):
+            return slice(PART * s, PART * (s + 1))
+
+        nc.sync.dma_start(wgs_sb[:, :HALF], wgs[:, :HALF])
+        nc.sync.dma_start(cap_sb[0][:, :HALF], cap[rows(0), :HALF])
+        idx2 = load_list(offs2, "idx2")
+        nc.sync.dma_start(page0_sb[0][:], page0[rows(0), :])
+        w1_raw[1] = load_w1(1)
+        nc.sync.dma_start(cap_sb[0][:, HALF:], cap[rows(0), HALF:])
+        nc.sync.dma_start(wgs_sb[:, HALF:], wgs[:, HALF:])
+
+        w1_q = {0: quantise_w1(0, w1_raw[0])}
+
+        v_sc = sb.tile([PART, S], U8, name="v_sc", align_bytes=64)
+        nc.vector.tensor_copy(v_sc[:], tab_sc[:].indirect(idx[:]))
+        v_w = []
+        for a in range(PASSES):
+            t = sb.tile([PART, S], U32, name="v_w%d" % a, tag="tab_sc" if a == PASSES - 1 else "v_w%d" % a, align_bytes=64)
+            if a < PASSES - 1:
+                nc.vector.tensor_copy(t[:], tab_w[a][:].indirect(idx[:]))
+            else:
+                for h in range(2):
+                    nc.vector.tensor_copy(
+                        t[:, HALF * h : HALF * (h + 1)], tab_w[a][:].indirect(entries(idx, HALF * h, HALF))
+                    )
+            v_w.append(t)
+
+        def first_product(s, h):
+            codes, scales = w1_q[s]
+            bank = psum.tile([PART, HALF], F32, name="h_bank", tag="acc", bufs=4)
+            cols = slice(HALF * h, HALF * (h + 1))
+            for a in range(PASSES):
+                nc.tensor.matmul_mx(
+                    bank[:],
+                    lhsT=codes[:, PART * a : PART * (a + 1)].bitcast(FP8X4),
+                    lhsT_scale=scales[:, PART * a : PART * (a + 1)],
+                    rhs=v_w[a][:, cols].bitcast(FP8X4),
+                    rhs_scale=v_sc[4 * a : PART, cols],
+                    start=(a == 0),
+                    stop=(a == PASSES - 1),
+                )
+            return bank
+
+        def factors(s, first, count):
+            t = sb.tile([PART, count], F32, name="factor", tag="factor%d" % (s % 2 if s < SLABS - 1 else 2), bufs=1)
+            nc.scalar.activation(t[:], wgs_sb[:, first : first + count], ACT.Copy, scale=gain_sb[:, s : s + 1])
+            return t
+
+        def put(page, list_tile, first, count, values, weights):
+            nc.vector.tensor_tensor(
+                page[:].indirect(entries(list_tile, first, count)), values, weights, ALU.mult
+            )
+
+        banks = [first_product(0, h) for h in range(2)]
+        fac0 = sb.tile([PART, S], F32, name="factor", tag="factor0", bufs=1)
+        nc.scalar.activation(fac0[:, :HALF], wgs_sb[:, :HALF], ACT.Copy, scale=gain_sb[:, 0:1])
+        nc.vector.tensor_tensor(cap_sb[0][:, :HALF], banks[0][:], cap_sb[0][:, :HALF], ALU.min)
+        put(page0_sb[0], idx2, 0, HALF, cap_sb[0][:, :HALF], fac0[:, :HALF])
+        w1_q[1] = quantise_w1(1, w1_raw[1])
+        nc.scalar.activation(fac0[:, HALF:], wgs_sb[:, HALF:], ACT.Copy, scale=gain_sb[:, 0:1])
+        limited = sb.tile([PART, HALF], F32, name="limited", tag="w1_bf1", align_bytes=64)
+        nc.vector.tensor_tensor(limited[:], banks[1][:], cap_sb[0][:, HALF:], ALU.min)
+        put(page0_sb[0], idx2, HALF, HALF, limited[:], fac0[:, HALF:])
+
+        nc.sync.dma_start(cap_sb[1][:], cap[rows(1), :])
+        w1_raw[2] = load_w1(2)
+        nc.sync.dma_start(page0_sb[1][:], page0[rows(1), :])
+        idx3 = load_list(offs3, "idx3")
+        base_sb = load_vector(base, "base_sb")
+        nc.sync.dma_start(cap_sb[2][:], cap[rows(2), :])
+        w1_raw[3] = load_w1(3)
+        nc.sync.dma_start(page0_sb[2][:], page0[rows(2), :])
+        w3_raw = sb.tile([PART, 4, N], F32, name="w3_raw")
+        nc.sync.dma_start(w3_raw[:], w3.rearrange("(p i) n -> p i n", i=4))
+        nc.sync.dma_start(cap_sb[3][:], cap[rows(3), :])
+        nc.sync.dma_start(page0_sb[3][:], page0[rows(3), :])
+        w2_w = sb.tile([PART, 2 * N], U8, name="w2_w", align_bytes=64)
+        nc.sync.dma_start(w2_w[:].bitcast(I32), w2_words[0].bitcast(I32))
+        for q in range(4):
+            nc.sync.dma_start(
+                w2_sc[32 * q : 32 * q + 4, :].bitcast(I32),
+                w2_scales[0, 4 * q : 4 * q + 4, :].bitcast(I32),
+            )
+        keep_sb = load_vector(keep, "keep_sb")
+        minus_keep = sb.tile([PART, SLABS], F32, name="minus_keep")
+        nc.scalar.activation(minus_keep[:], keep_sb[:], ACT.Copy, scale=-1.0)
+        idx4 = load_list(offs4, "idx4")
+        wgo_sb = sb.tile([PART, P], F32, name="wgo_sb")
+        nc.sync.dma_start(wgo_sb[:], wgo)
+        page1_sb = []
+        for s in range(SLABS):
+            t = sb.tile([PART, T2], F32, name="page1_sb", tag="big%d" % s, align_bytes=64)
+            nc.sync.dma_start(t[:], page1[rows(s), :])
+            page1_sb.append(t)
+
+        x = {}
+        xt_banks = {}
+
+        def fetch(c, s, dst):
+            nc.vector.tensor_copy(dst, page0_sb[s][:].indirect(entries(idx3, CHUNK * c, CHUNK)))
+            x[c, s] = dst
+
+        def turn(c, s):
+            dst = x[c, s]
+            nc.scalar.activation(dst, dst, ACT.Identity, bias=base_sb[:, s : s + 1])
+            if s % 2 == 0:
+                xt_banks[c, s // 2] = psum.tile([PART, 2, 2 * PART], F32, name="xt_bank", tag="xt%d" % (s // 2))
+            bank = xt_banks[c, s // 2]
+            for jt in range(2):
+                nc.tensor.transpose(
+                    bank[:, jt, PART * (s % 2) : PART * (s % 2 + 1)], dst[:, PART * jt : PART * (jt + 1)], ident[:]
+                )
+
+        xt_bf = {}
+
+        def round_pair(c, pair):
+            if pair == 0:
+                xt_bf[c] = sb.tile([PART, 2, H], BF16, name="xt_bf", tag="xt_bf", bufs=2)
+            nc.scalar.copy(xt_bf[c][:, :, 2 * PART * pair : 2 * PART * (pair + 1)], xt_banks[c, pair][:])
+
+        for s in range(1, SLABS):
+            banks = [first_product(s, h) for h in range(2)]
+            fac = factors(s, 0, S)
+            if s < SLABS - 1:
+                w1_q[s + 1] = quantise_w1(s + 1, w1_raw[s + 1])
+                limited = sb.tile([PART, S], F32, name="limited", tag="w1_bf%d" % (s + 1), align_bytes=64)
+            else:
+                w3_bf = sb.tile([PART, 4 * N], BF16, name="w3_bf", tag="w3_bf", align_bytes=64)
+                interleave(nc.scalar.copy, w3_bf[:], w3_raw[:])
+                w3_codes = sb.tile([PART, N], U32, name="w3_codes", align_bytes=64)
+                w3_sc = sb.tile([PART, N], U8, name="w3_sc", align_bytes=64)
+                nc.vector.quantize_mx(w3_codes[:].bitcast(FP8X4), w3_sc[:], w3_bf[:])
+                limited = sb.tile([PART, S], F32, name="limited", tag="w3_bf", align_bytes=64)
+            for h in range(2):
+                cols = slice(HALF * h, HALF * (h + 1))
+                nc.vector.tensor_tensor(limited[:, cols], banks[h][:], cap_sb[s][:, cols], ALU.min)
+            fetch(0, s - 1, cap_sb[s][:, :CHUNK])
+            put(page0_sb[s], idx2, 0, S, limited[:], fac[:])
+            turn(0, s - 1)
+            if s == 2:
+                round_pair(0, 0)
+        fetch(0, SLABS - 1, cap_sb[SLABS - 1][:, HALF : HALF + CHUNK])
+        turn(0, SLABS - 1)
+        round_pair(0, 1)
+
+        x_codes = sb.tile([PART, P], U32, name="x_codes", align_bytes=64)
+        x_sc = sb.tile([PART, P], U8, name="x_sc", align_bytes=64)
+
+        def quantise_x(c):
+            words = xt_bf[c][:].rearrange("p t r -> p (t r)").bitcast(F32)
+            bank = psum.tile([PART, 2, 2, PART], F32, name="word_bank", tag="words")
+            for jt in range(2):
+                for u in range(2):
+                    nc.tensor.transpose(bank[:, jt, u, :], words[:, 256 * jt + u : 256 * (jt + 1) : 2], ident[:])
+            grouped = sb.tile([PART, 4 * CHUNK], BF16, name="grouped", tag="grouped%d" % min(c, 1), bufs=1 if c == 0 else 2, align_bytes=64)
+            nc.scalar.copy(
+                grouped[:].bitcast(F32).rearrange("p (t j u) -> p t j u", t=2, u=2),
+                bank[:].rearrange("p t u j -> p t j u"),
+            )
+            cols = slice(CHUNK * c, CHUNK * (c + 1))
+            nc.vector.quantize_mx(x_codes[:, cols].bitcast(FP8X4), x_sc[:, cols], grouped[:])
+
+        def second_products(c, pair):
+            width = 2 * PART
+            outs = slice(width * pair, width * (pair + 1))
+            parts = []
+            for w, w_scale, func in (
+                (w2_w[:, 2 * width * pair : 2 * width * (pair + 1)].bitcast(FP4X4), w2_sc, ACT.Tanh),
+                (w3_codes[:, outs].bitcast(FP8X4), w3_sc, ACT.Copy),
+            ):
+                bank = psum.tile([PART, 2, width], F32, name="p_bank", tag="acc", bufs=4)
+                for jt in range(2):
+                    cols = slice(CHUNK * c + PART * jt, CHUNK * c + PART * (jt + 1))
+                    nc.tensor.matmul_mx(
+                        bank[:, jt, :], lhsT=x_codes[:, cols].bitcast(FP8X4), lhsT_scale=x_sc[:, cols],
+                        rhs=w, rhs_scale=w_scale[:, outs], start=True, stop=True,
+                    )
+                part = sb.tile([PART, 2, width], F32, name="part", tag="part", bufs=4)
+                nc.scalar.activation(part[:], bank[:], func)
+                parts.append(part)
+            return parts
+
+        def finish(c, pair, parts, tag):
+            y_bank = psum.tile([PART, 2, CHUNK], F32, name="y_bank", tag=tag)
+            for i in range(2):
+                for jt in range(2):
+                    for k in range(2):
+                        nc.tensor.matmul(
+                            y_bank[:, i, PART * jt : PART * (jt + 1)],
+                            lhsT=parts[k][:, jt, PART * i : PART * (i + 1)], rhs=ident[:],
+                            is_transpose=True, start=(k == 0), stop=(k == 1),
+                        )
+            for i in range(2):
+                s = 2 * pair + i
+                nc.vector.scalar_tensor_tensor(
+                    x[c, s], x[c, s], minus_keep[:, s : s + 1], y_bank[:, i, :], ALU.mult, ALU.add
+                )
+            for i in range(2):
+                s = 2 * pair + i
+                put(page1_sb[s], idx4, CHUNK * c, CHUNK, x[c, s], wgo_sb[:, CHUNK * c : CHUNK * (c + 1)])
+                if c == CHUNKS - 1:
+                    nc.sync.dma_start(out[rows(s), :], page1_sb[s][:])
+
+        def front(c):
+            for s in range(SLABS):
+                turn(c, s)
+                if s % 2 == 1:
+                    round_pair(c, s // 2)
+            quantise_x(c)
+
+        for s in range(SLABS):
+            fetch(1, s, limited[:, CHUNK * s : CHUNK * (s + 1)])
+        for s in range(2):
+            fetch(2, s, fac[:, CHUNK * s : CHUNK * (s + 1)])
+        quantise_x(0)
+        late = [(2, 2), (2, 3)] + [(3, s) for s in range(SLABS)]
+        x_late = sb.tile([PART, len(late), CHUNK], F32, name="x_late", tag="grouped0", align_bytes=64)
+        for i, (c, s) in enumerate(late):
+            fetch(c, s, x_late[:, i, :])
+        for c in range(CHUNKS):
+            parts = second_products(c, 0)
+            finish(c, 0, parts, "y")
+            parts = second_products(c, 1)
+            if c + 1 < CHUNKS:
+                front(c + 1)
+            finish(c, 1, parts, "words")

@@ -51,11 +51,6 @@ def tile_list_cork_batch_page_kernel(
         make_identity(nc, ident[:])
         tab_sc = sb.tile([PART, T], U8, name="tab_sc", tag="tab_sc", align_bytes=64)
         nc.vector.memset(tab_sc[:].bitcast(I32), 0)
-        for q in range(4):
-            nc.gpsimd.dma_start(
-                tab_sc[32 * q : 32 * q + 4 * PASSES, :].bitcast(I32),
-                tab_scales[:, 4 * q : 4 * q + 4, :].bitcast(I32),
-            )
         w2_sc = sb.tile([PART, N], U8, name="w2_sc", align_bytes=64)
         nc.vector.memset(w2_sc[:].bitcast(I32), 0)
 
@@ -84,7 +79,7 @@ def tile_list_cork_batch_page_kernel(
 
         def quantise_w1(s, raws):
             copy = nc.vector.tensor_copy if s == 0 else nc.scalar.copy
-            codes = sb.tile([PART, PASSES * PART], U32, name="w1_codes%d" % s, align_bytes=64)
+            codes = sb.tile([PART, PASSES * PART], U32, name="w1_codes", tag="w1_codes%d" % s, align_bytes=64)
             scales = sb.tile([PART, PASSES * PART], U8, name="w1_scales%d" % s, align_bytes=64)
             for lo, hi, tag in ((0, 2, "w1_bf%d" % s), (2, 3, "w1_bf_last")):
                 grouped = sb.tile([PART, 512 * (hi - lo)], BF16, name="w1_bf", tag=tag, align_bytes=64)
@@ -96,26 +91,34 @@ def tile_list_cork_batch_page_kernel(
             return codes, scales
 
         idx = load_list(offs, "idx")
-        w1_raw = {0: load_w1(0)}
         tab_w = []
+        w1_raw = {}
         for a in range(PASSES):
             t = sb.tile([PART, T], U32, name="tab_w", tag="big%d" % a, align_bytes=64)
             nc.sync.dma_start(t[:].bitcast(I32), tab_words[a].rearrange("p t i -> p (t i)").bitcast(I32))
             tab_w.append(t)
+            if a == 0:
+                for q in range(4):
+                    nc.sync.dma_start(
+                        tab_sc[32 * q : 32 * q + 4 * PASSES, :].bitcast(I32),
+                        tab_scales[:, 4 * q : 4 * q + 4, :].bitcast(I32),
+                    )
+                w1_raw[0] = load_w1(0)
         gain_sb = load_vector(gain, "gain_sb")
         wgs_sb = sb.tile([PART, S], F32, name="wgs_sb")
-        cap_sb = [sb.tile([PART, S], F32, name="cap_sb%d" % s) for s in range(SLABS)]
+        cap_first = [sb.tile([PART, HALF], F32, name="cap_first", tag="w1_codes%d" % (h + 1), align_bytes=64) for h in range(2)]
+        cap_sb = {s: sb.tile([PART, S], F32, name="cap_sb%d" % s) for s in range(1, SLABS)}
         page0_sb = [sb.tile([PART, T2], F32, name="page0_sb%d" % s) for s in range(SLABS)]
 
         def rows(s):
             return slice(PART * s, PART * (s + 1))
 
         nc.sync.dma_start(wgs_sb[:, :HALF], wgs[:, :HALF])
-        nc.sync.dma_start(cap_sb[0][:, :HALF], cap[rows(0), :HALF])
+        nc.sync.dma_start(cap_first[0][:], cap[rows(0), :HALF])
         idx2 = load_list(offs2, "idx2")
         nc.sync.dma_start(page0_sb[0][:], page0[rows(0), :])
         w1_raw[1] = load_w1(1)
-        nc.sync.dma_start(cap_sb[0][:, HALF:], cap[rows(0), HALF:])
+        nc.sync.dma_start(cap_first[1][:], cap[rows(0), HALF:])
         nc.sync.dma_start(wgs_sb[:, HALF:], wgs[:, HALF:])
 
         w1_q = {0: quantise_w1(0, w1_raw[0])}
@@ -163,12 +166,13 @@ def tile_list_cork_batch_page_kernel(
         banks = [first_product(0, h) for h in range(2)]
         fac0 = sb.tile([PART, S], F32, name="factor", tag="factor0", bufs=1)
         nc.scalar.activation(fac0[:, :HALF], wgs_sb[:, :HALF], ACT.Copy, scale=gain_sb[:, 0:1])
-        nc.vector.tensor_tensor(cap_sb[0][:, :HALF], banks[0][:], cap_sb[0][:, :HALF], ALU.min)
-        put(page0_sb[0], idx2, 0, HALF, cap_sb[0][:, :HALF], fac0[:, :HALF])
+        limited = sb.tile([PART, HALF], F32, name="limited", tag="limited_first")
+        nc.vector.tensor_tensor(limited[:], banks[0][:], cap_first[0][:], ALU.min)
+        put(page0_sb[0], idx2, 0, HALF, limited[:], fac0[:, :HALF])
         w1_q[1] = quantise_w1(1, w1_raw[1])
         nc.scalar.activation(fac0[:, HALF:], wgs_sb[:, HALF:], ACT.Copy, scale=gain_sb[:, 0:1])
         limited = sb.tile([PART, HALF], F32, name="limited", tag="w1_bf1", align_bytes=64)
-        nc.vector.tensor_tensor(limited[:], banks[1][:], cap_sb[0][:, HALF:], ALU.min)
+        nc.vector.tensor_tensor(limited[:], banks[1][:], cap_first[1][:], ALU.min)
         put(page0_sb[0], idx2, HALF, HALF, limited[:], fac0[:, HALF:])
 
         nc.sync.dma_start(cap_sb[1][:], cap[rows(1), :])
@@ -203,30 +207,31 @@ def tile_list_cork_batch_page_kernel(
             page1_sb.append(t)
 
         x = {}
-        xt_banks = {}
-
-        def fetch(c, s, dst):
-            nc.vector.tensor_copy(dst, page0_sb[s][:].indirect(entries(idx3, CHUNK * c, CHUNK)))
-            x[c, s] = dst
-
-        def turn(c, s):
-            dst = x[c, s]
-            nc.scalar.activation(dst, dst, ACT.Identity, bias=base_sb[:, s : s + 1])
-            if s % 2 == 0:
-                xt_banks[c, s // 2] = psum.tile([PART, 2, 2 * PART], F32, name="xt_bank", tag="xt%d" % (s // 2))
-            bank = xt_banks[c, s // 2]
-            for jt in range(2):
-                nc.tensor.transpose(
-                    bank[:, jt, PART * (s % 2) : PART * (s % 2 + 1)], dst[:, PART * jt : PART * (jt + 1)], ident[:]
-                )
-
         xt_bf = {}
 
-        def round_pair(c, pair):
+        def fetch(first, count, s, dst):
+            nc.vector.tensor_copy(dst, page0_sb[s][:].indirect(entries(idx3, first, count)))
+            for c in range(first // CHUNK, (first + count) // CHUNK):
+                x[c, s] = dst[:, CHUNK * c - first : CHUNK * (c + 1) - first]
+
+        def add_base(values, s):
+            nc.scalar.activation(values, values, ACT.Identity, bias=base_sb[:, s : s + 1])
+
+        def turn(bank, c, s):
+            for jt in range(2):
+                nc.tensor.transpose(
+                    bank[:, jt, PART * (s % 2) : PART * (s % 2 + 1)], x[c, s][:, PART * jt : PART * (jt + 1)], ident[:]
+                )
+
+        def pair_bank(pair):
+            return psum.tile([PART, 2, 2 * PART], F32, name="xt_bank", tag="xt%d" % pair)
+
+        def round_pair(c, pair, bank):
             if pair == 0:
                 xt_bf[c] = sb.tile([PART, 2, H], BF16, name="xt_bf", tag="xt_bf", bufs=2)
-            nc.scalar.copy(xt_bf[c][:, :, 2 * PART * pair : 2 * PART * (pair + 1)], xt_banks[c, pair][:])
+            nc.scalar.copy(xt_bf[c][:, :, 2 * PART * pair : 2 * PART * (pair + 1)], bank[:])
 
+        first_banks = [pair_bank(pair) for pair in range(2)]
         for s in range(1, SLABS):
             banks = [first_product(s, h) for h in range(2)]
             fac = factors(s, 0, S)
@@ -243,21 +248,24 @@ def tile_list_cork_batch_page_kernel(
             for h in range(2):
                 cols = slice(HALF * h, HALF * (h + 1))
                 nc.vector.tensor_tensor(limited[:, cols], banks[h][:], cap_sb[s][:, cols], ALU.min)
-            fetch(0, s - 1, cap_sb[s][:, :CHUNK])
+            fetch(0, CHUNK, s - 1, cap_sb[s][:, :CHUNK])
             put(page0_sb[s], idx2, 0, S, limited[:], fac[:])
-            turn(0, s - 1)
+            add_base(x[0, s - 1], s - 1)
+            turn(first_banks[(s - 1) // 2], 0, s - 1)
             if s == 2:
-                round_pair(0, 0)
-        fetch(0, SLABS - 1, cap_sb[SLABS - 1][:, HALF : HALF + CHUNK])
-        turn(0, SLABS - 1)
-        round_pair(0, 1)
+                round_pair(0, 0, first_banks[0])
+        last = SLABS - 1
+        fetch(0, CHUNK, last, cap_sb[last][:, HALF : HALF + CHUNK])
+        add_base(x[0, last], last)
+        turn(first_banks[1], 0, last)
+        round_pair(0, 1, first_banks[1])
 
         x_codes = sb.tile([PART, P], U32, name="x_codes", align_bytes=64)
         x_sc = sb.tile([PART, P], U8, name="x_sc", align_bytes=64)
 
-        def quantise_x(c):
+        def quantise_x(c, tag):
             words = xt_bf[c][:].rearrange("p t r -> p (t r)").bitcast(F32)
-            bank = psum.tile([PART, 2, 2, PART], F32, name="word_bank", tag="words")
+            bank = psum.tile([PART, 2, 2, PART], F32, name="word_bank", tag=tag)
             for jt in range(2):
                 for u in range(2):
                     nc.tensor.transpose(bank[:, jt, u, :], words[:, 256 * jt + u : 256 * (jt + 1) : 2], ident[:])
@@ -284,7 +292,7 @@ def tile_list_cork_batch_page_kernel(
                         bank[:, jt, :], lhsT=x_codes[:, cols].bitcast(FP8X4), lhsT_scale=x_sc[:, cols],
                         rhs=w, rhs_scale=w_scale[:, outs], start=True, stop=True,
                     )
-                part = sb.tile([PART, 2, width], F32, name="part", tag="part", bufs=4)
+                part = sb.tile([PART, 2, width], F32, name="part", tag="part", bufs=12)
                 nc.scalar.activation(part[:], bank[:], func)
                 parts.append(part)
             return parts
@@ -307,29 +315,61 @@ def tile_list_cork_batch_page_kernel(
             for i in range(2):
                 s = 2 * pair + i
                 put(page1_sb[s], idx4, CHUNK * c, CHUNK, x[c, s], wgo_sb[:, CHUNK * c : CHUNK * (c + 1)])
-                if c == CHUNKS - 1:
-                    nc.sync.dma_start(out[rows(s), :], page1_sb[s][:])
 
-        def front(c):
-            for s in range(SLABS):
-                turn(c, s)
-                if s % 2 == 1:
-                    round_pair(c, s // 2)
-            quantise_x(c)
+        def front(c, tag):
+            for pair in range(2):
+                bank = pair_bank(pair)
+                for s in (2 * pair, 2 * pair + 1):
+                    if c < 3:
+                        add_base(x[c, s] if c == 1 else wide[s], s)
+                    turn(bank, c, s)
+                round_pair(c, pair, bank)
+            quantise_x(c, tag)
 
         for s in range(SLABS):
-            fetch(1, s, limited[:, CHUNK * s : CHUNK * (s + 1)])
+            fetch(CHUNK, CHUNK, s, limited[:, CHUNK * s : CHUNK * (s + 1)])
+        wide = {s: fac[:, HALF * s : HALF * (s + 1)] for s in range(2)}
         for s in range(2):
-            fetch(2, s, fac[:, CHUNK * s : CHUNK * (s + 1)])
-        quantise_x(0)
-        late = [(2, 2), (2, 3)] + [(3, s) for s in range(SLABS)]
-        x_late = sb.tile([PART, len(late), CHUNK], F32, name="x_late", tag="grouped0", align_bytes=64)
-        for i, (c, s) in enumerate(late):
-            fetch(c, s, x_late[:, i, :])
-        for c in range(CHUNKS):
-            parts = second_products(c, 0)
-            finish(c, 0, parts, "y")
-            parts = second_products(c, 1)
-            if c + 1 < CHUNKS:
-                front(c + 1)
-            finish(c, 1, parts, "words")
+            fetch(HALF, HALF, s, wide[s])
+        quantise_x(0, "words")
+        x_late = sb.tile([PART, 2, HALF], F32, name="x_late", tag="grouped0", align_bytes=64)
+        for s in range(2, SLABS):
+            wide[s] = x_late[:, s - 2, :]
+            fetch(HALF, HALF, s, wide[s])
+
+        parts = [second_products(0, pair) for pair in range(2)]
+        front(1, "words")
+        finish(0, 0, parts[0], "words")
+        finish(0, 1, parts[1], "y")
+        parts = [second_products(1, pair) for pair in range(2)]
+        front(2, "words")
+        finish(1, 0, parts[0], "words")
+        front(3, "y")
+        finish(1, 1, parts[1], "y")
+
+        for pair in range(2):
+            slabs = (2 * pair, 2 * pair + 1)
+            parts = {}
+            for s in slabs:
+                nc.scalar.activation(wide[s], wide[s], ACT.Copy, scale=minus_keep[:, s : s + 1])
+            for c in (2, 3):
+                bank = pair_bank(c % 2)
+                for s in slabs:
+                    turn(bank, c, s)
+                own = sb.tile([PART, 2, 2 * PART], F32, name="part", tag="part", bufs=12)
+                nc.scalar.copy(own[:], bank[:])
+                parts[c] = [own]
+            for c in (2, 3):
+                parts[c] = parts[c] + second_products(c, pair)
+            for i, s in enumerate(slabs):
+                y_bank = psum.tile([PART, HALF], F32, name="y_bank", tag=("words", "y")[i])
+                for t in range(4):
+                    for k in range(3):
+                        nc.tensor.matmul(
+                            y_bank[:, PART * t : PART * (t + 1)],
+                            lhsT=parts[2 + t // 2][k][:, t % 2, PART * i : PART * (i + 1)], rhs=ident[:],
+                            is_transpose=True, start=(k == 0), stop=(k == 2),
+                        )
+                nc.scalar.copy(wide[s], y_bank[:])
+                put(page1_sb[s], idx4, HALF, HALF, wide[s], wgo_sb[:, HALF:])
+                nc.sync.dma_start(out[rows(s), :], page1_sb[s][:])

@@ -47,18 +47,20 @@ def tile_list_cork_batch_page_kernel(
         nc.vector.memset(warm[:, 0:1], 0.0)
         nc.scalar.activation(warm[:, 4:5], warm[:, 0:1], ACT.Tanh)
 
+        vec_rows = sb.tile([PART, PART], F32, name="vec_rows")
+        nc.gpsimd.memset(vec_rows[:], 0.0)
         ident = sb.tile([PART, PART], F32, name="ident")
         make_identity(nc, ident[:])
         tab_sc = sb.tile([PART, T], U8, name="tab_sc", tag="tab_sc", align_bytes=64)
         nc.vector.memset(tab_sc[:].bitcast(I32), 0)
+        for q in range(4):
+            nc.gpsimd.dma_start(
+                tab_sc[32 * q : 32 * q + 4 * PASSES, :].bitcast(I32),
+                tab_scales[:, 4 * q : 4 * q + 4, :].bitcast(I32),
+            )
         w2_sc = sb.tile([PART, N], U8, name="w2_sc", align_bytes=64)
         nc.vector.memset(w2_sc[:].bitcast(I32), 0)
 
-        def load_vector(vec, name):
-            t = sb.tile([PART, SLABS], F32, name=name)
-            with nc.allow_non_contiguous_dma(reason="one value for each partition and slab"):
-                nc.sync.dma_start(t[:], vec.rearrange("(s p) -> p s", p=PART))
-            return t
 
         def interleave(copy, dst, src):
             copy(
@@ -70,7 +72,7 @@ def tile_list_cork_batch_page_kernel(
             raws = []
             for a in range(PASSES):
                 raw = sb.tile([PART, 4, PART], F32, name="w1_raw", tag="w1_raw", bufs=2 * PASSES)
-                nc.sync.dma_start(
+                (nc.scalar if s == 0 else nc.sync).dma_start(
                     raw[:],
                     w1[512 * a : 512 * (a + 1), PART * s : PART * (s + 1)].rearrange("(p i) c -> p i c", i=4),
                 )
@@ -91,20 +93,22 @@ def tile_list_cork_batch_page_kernel(
             return codes, scales
 
         idx = load_list(offs, "idx")
+        w1_raw = {0: load_w1(0)}
         tab_w = []
-        w1_raw = {}
         for a in range(PASSES):
             t = sb.tile([PART, T], U32, name="tab_w", tag="big%d" % a, align_bytes=64)
             nc.sync.dma_start(t[:].bitcast(I32), tab_words[a].rearrange("p t i -> p (t i)").bitcast(I32))
             tab_w.append(t)
             if a == 0:
-                for q in range(4):
-                    nc.sync.dma_start(
-                        tab_sc[32 * q : 32 * q + 4 * PASSES, :].bitcast(I32),
-                        tab_scales[:, 4 * q : 4 * q + 4, :].bitcast(I32),
-                    )
-                w1_raw[0] = load_w1(0)
-        gain_sb = load_vector(gain, "gain_sb")
+                for i, vec in enumerate((gain, base, keep)):
+                    nc.sync.dma_start(vec_rows[SLABS * i : SLABS * (i + 1), :], vec.rearrange("(s p) -> s p", p=PART))
+        vec_bank = psum.tile([PART, PART], F32, name="vec_bank", tag="y")
+        nc.tensor.transpose(vec_bank[:], vec_rows[:], ident[:])
+        vec_cols = sb.tile([PART, 2 * SLABS], F32, name="vec_cols")
+        nc.scalar.copy(vec_cols[:], vec_bank[:, : 2 * SLABS])
+        gain_sb, base_sb = vec_cols[:, :SLABS], vec_cols[:, SLABS:]
+        minus_keep = sb.tile([PART, SLABS], F32, name="minus_keep")
+        nc.scalar.activation(minus_keep[:], vec_bank[:, 2 * SLABS : 3 * SLABS], ACT.Copy, scale=-1.0)
         wgs_sb = sb.tile([PART, S], F32, name="wgs_sb")
         cap_first = [sb.tile([PART, HALF], F32, name="cap_first", tag="w1_codes%d" % (h + 1), align_bytes=64) for h in range(2)]
         cap_sb = {s: sb.tile([PART, S], F32, name="cap_sb%d" % s) for s in range(1, SLABS)}
@@ -179,7 +183,6 @@ def tile_list_cork_batch_page_kernel(
         w1_raw[2] = load_w1(2)
         nc.sync.dma_start(page0_sb[1][:], page0[rows(1), :])
         idx3 = load_list(offs3, "idx3")
-        base_sb = load_vector(base, "base_sb")
         nc.sync.dma_start(cap_sb[2][:], cap[rows(2), :])
         w1_raw[3] = load_w1(3)
         nc.sync.dma_start(page0_sb[2][:], page0[rows(2), :])
@@ -194,9 +197,6 @@ def tile_list_cork_batch_page_kernel(
                 w2_sc[32 * q : 32 * q + 4, :].bitcast(I32),
                 w2_scales[0, 4 * q : 4 * q + 4, :].bitcast(I32),
             )
-        keep_sb = load_vector(keep, "keep_sb")
-        minus_keep = sb.tile([PART, SLABS], F32, name="minus_keep")
-        nc.scalar.activation(minus_keep[:], keep_sb[:], ACT.Copy, scale=-1.0)
         idx4 = load_list(offs4, "idx4")
         wgo_sb = sb.tile([PART, P], F32, name="wgo_sb")
         nc.sync.dma_start(wgo_sb[:], wgo)
@@ -226,10 +226,14 @@ def tile_list_cork_batch_page_kernel(
         def pair_bank(pair):
             return psum.tile([PART, 2, 2 * PART], F32, name="xt_bank", tag="xt%d" % pair)
 
-        def round_pair(c, pair, bank):
-            if pair == 0:
-                xt_bf[c] = sb.tile([PART, 2, H], BF16, name="xt_bf", tag="xt_bf", bufs=2)
-            nc.scalar.copy(xt_bf[c][:, :, 2 * PART * pair : 2 * PART * (pair + 1)], bank[:])
+        def round_slabs(c, first, count, bank):
+            if first == 0:
+                xt_bf[c] = sb.tile([PART, 2, 2, 2 * PART], BF16, name="xt_bf", tag="xt_bf", bufs=2)
+            lo = PART * (first % 2)
+            nc.scalar.copy(
+                xt_bf[c][:, :, :, 64 * first : 64 * (first + count)].rearrange("p t u (q e) -> p t u q e", e=2),
+                bank[:, :, lo : lo + PART * count].rearrange("p t (q u e) -> p t u q e", u=2, e=2),
+            )
 
         first_banks = [pair_bank(pair) for pair in range(2)]
         for s in range(1, SLABS):
@@ -253,22 +257,24 @@ def tile_list_cork_batch_page_kernel(
             add_base(x[0, s - 1], s - 1)
             turn(first_banks[(s - 1) // 2], 0, s - 1)
             if s == 2:
-                round_pair(0, 0, first_banks[0])
+                round_slabs(0, 0, 2, first_banks[0])
+            if s == 3:
+                round_slabs(0, 2, 1, first_banks[1])
         last = SLABS - 1
         fetch(0, CHUNK, last, cap_sb[last][:, HALF : HALF + CHUNK])
         add_base(x[0, last], last)
         turn(first_banks[1], 0, last)
-        round_pair(0, 1, first_banks[1])
+        round_slabs(0, last, 1, first_banks[1])
 
         x_codes = sb.tile([PART, P], U32, name="x_codes", align_bytes=64)
         x_sc = sb.tile([PART, P], U8, name="x_sc", align_bytes=64)
 
         def quantise_x(c, tag):
-            words = xt_bf[c][:].rearrange("p t r -> p (t r)").bitcast(F32)
+            words = xt_bf[c][:].rearrange("p t u r -> p (t u r)").bitcast(F32)
             bank = psum.tile([PART, 2, 2, PART], F32, name="word_bank", tag=tag)
             for jt in range(2):
                 for u in range(2):
-                    nc.tensor.transpose(bank[:, jt, u, :], words[:, 256 * jt + u : 256 * (jt + 1) : 2], ident[:])
+                    nc.tensor.transpose(bank[:, jt, u, :], words[:, PART * (2 * jt + u) : PART * (2 * jt + u + 1)], ident[:])
             grouped = sb.tile([PART, 4 * CHUNK], BF16, name="grouped", tag="grouped%d" % min(c, 1), bufs=1 if c == 0 else 2, align_bytes=64)
             nc.scalar.copy(
                 grouped[:].bitcast(F32).rearrange("p (t j u) -> p t j u", t=2, u=2),
@@ -277,12 +283,12 @@ def tile_list_cork_batch_page_kernel(
             cols = slice(CHUNK * c, CHUNK * (c + 1))
             nc.vector.quantize_mx(x_codes[:, cols].bitcast(FP8X4), x_sc[:, cols], grouped[:])
 
-        def second_products(c, pair):
-            width = 2 * PART
-            outs = slice(width * pair, width * (pair + 1))
+        def second_products(c, first, count):
+            width = PART * count
+            outs = slice(PART * first, PART * (first + count))
             parts = []
             for w, w_scale, func in (
-                (w2_w[:, 2 * width * pair : 2 * width * (pair + 1)].bitcast(FP4X4), w2_sc, ACT.Tanh),
+                (w2_w[:, 2 * outs.start : 2 * outs.stop].bitcast(FP4X4), w2_sc, ACT.Tanh),
                 (w3_codes[:, outs].bitcast(FP8X4), w3_sc, ACT.Copy),
             ):
                 bank = psum.tile([PART, 2, width], F32, name="p_bank", tag="acc", bufs=4)
@@ -292,28 +298,29 @@ def tile_list_cork_batch_page_kernel(
                         bank[:, jt, :], lhsT=x_codes[:, cols].bitcast(FP8X4), lhsT_scale=x_sc[:, cols],
                         rhs=w, rhs_scale=w_scale[:, outs], start=True, stop=True,
                     )
-                part = sb.tile([PART, 2, width], F32, name="part", tag="part", bufs=12)
+                part = sb.tile([PART, 2, width], F32, name="part", tag="part", bufs=10)
                 nc.scalar.activation(part[:], bank[:], func)
                 parts.append(part)
             return parts
 
-        def finish(c, pair, parts, tag):
-            y_bank = psum.tile([PART, 2, CHUNK], F32, name="y_bank", tag=tag)
-            for i in range(2):
-                for jt in range(2):
-                    for k in range(2):
-                        nc.tensor.matmul(
-                            y_bank[:, i, PART * jt : PART * (jt + 1)],
-                            lhsT=parts[k][:, jt, PART * i : PART * (i + 1)], rhs=ident[:],
-                            is_transpose=True, start=(k == 0), stop=(k == 1),
-                        )
-            for i in range(2):
-                s = 2 * pair + i
-                nc.vector.scalar_tensor_tensor(
-                    x[c, s], x[c, s], minus_keep[:, s : s + 1], y_bank[:, i, :], ALU.mult, ALU.add
+        def add_turned(dst, parts, jt, i):
+            for k, part in enumerate(parts):
+                nc.tensor.matmul(
+                    dst, lhsT=part[:, jt, PART * i : PART * (i + 1)], rhs=ident[:],
+                    is_transpose=True, start=(k == 0), stop=(k == len(parts) - 1),
                 )
-            for i in range(2):
-                s = 2 * pair + i
+
+        def subtract_own(values, s, sums):
+            nc.vector.scalar_tensor_tensor(values, values, minus_keep[:, s : s + 1], sums, ALU.mult, ALU.add)
+
+        def finish(c, first, count, parts, tag):
+            y_bank = psum.tile([PART, count, CHUNK], F32, name="y_bank", tag=tag)
+            for i in range(count):
+                for jt in range(2):
+                    add_turned(y_bank[:, i, PART * jt : PART * (jt + 1)], parts, jt, i)
+            for i in range(count):
+                subtract_own(x[c, first + i], first + i, y_bank[:, i, :])
+            for s in range(first, first + count):
                 put(page1_sb[s], idx4, CHUNK * c, CHUNK, x[c, s], wgo_sb[:, CHUNK * c : CHUNK * (c + 1)])
 
         def front(c, tag):
@@ -323,7 +330,7 @@ def tile_list_cork_batch_page_kernel(
                     if c < 3:
                         add_base(x[c, s] if c == 1 else wide[s], s)
                     turn(bank, c, s)
-                round_pair(c, pair, bank)
+                round_slabs(c, 2 * pair, 2, bank)
             quantise_x(c, tag)
 
         for s in range(SLABS):
@@ -337,39 +344,55 @@ def tile_list_cork_batch_page_kernel(
             wide[s] = x_late[:, s - 2, :]
             fetch(HALF, HALF, s, wide[s])
 
-        parts = [second_products(0, pair) for pair in range(2)]
+        sums = []
+        for w, w_scale in (
+            (w3_codes[:, :PART].bitcast(FP8X4), w3_sc),
+            (w2_w[:, : 2 * PART].bitcast(FP4X4), w2_sc),
+        ):
+            bank = psum.tile([PART, CHUNK], F32, name="p_bank", tag="acc", bufs=4)
+            nc.tensor.matmul_mx(
+                bank[:], lhsT=w, lhsT_scale=w_scale[:, :PART],
+                rhs=x_codes[:, :CHUNK].bitcast(FP8X4), rhs_scale=x_sc[:, :CHUNK], start=True, stop=True,
+            )
+            sums.append(bank)
+        bounded = sb.tile([PART, CHUNK], F32, name="bounded", tag="part", bufs=10)
+        nc.scalar.activation(bounded[:], sums[1][:], ACT.Tanh)
+        subtract_own(x[0, 0], 0, sums[0][:])
+        nc.vector.tensor_tensor(x[0, 0], x[0, 0], bounded[:], ALU.add)
+        put(page1_sb[0], idx4, 0, CHUNK, x[0, 0], wgo_sb[:, :CHUNK])
+
+        parts = [second_products(0, 1, 1), second_products(0, 2, 2)]
         front(1, "words")
-        finish(0, 0, parts[0], "words")
-        finish(0, 1, parts[1], "y")
-        parts = [second_products(1, pair) for pair in range(2)]
+        finish(0, 1, 1, parts[0], "words")
+        finish(0, 2, 2, parts[1], "y")
+        parts = [second_products(1, 2 * pair, 2) for pair in range(2)]
         front(2, "words")
-        finish(1, 0, parts[0], "words")
+        finish(1, 0, 2, parts[0], "words")
         front(3, "y")
-        finish(1, 1, parts[1], "y")
+        finish(1, 2, 2, parts[1], "y")
 
         for pair in range(2):
             slabs = (2 * pair, 2 * pair + 1)
-            parts = {}
-            for s in slabs:
-                nc.scalar.activation(wide[s], wide[s], ACT.Copy, scale=minus_keep[:, s : s + 1])
-            for c in (2, 3):
-                bank = pair_bank(c % 2)
+            parts = {2: [], 3: []}
+            if pair == 1:
                 for s in slabs:
-                    turn(bank, c, s)
-                own = sb.tile([PART, 2, 2 * PART], F32, name="part", tag="part", bufs=12)
-                nc.scalar.copy(own[:], bank[:])
-                parts[c] = [own]
+                    nc.scalar.activation(wide[s], wide[s], ACT.Copy, scale=minus_keep[:, s : s + 1])
+                for c in (2, 3):
+                    bank = pair_bank(c % 2)
+                    for s in slabs:
+                        turn(bank, c, s)
+                    own = sb.tile([PART, 2, 2 * PART], F32, name="part", tag="part", bufs=10)
+                    nc.scalar.copy(own[:], bank[:])
+                    parts[c].append(own)
             for c in (2, 3):
-                parts[c] = parts[c] + second_products(c, pair)
+                parts[c].extend(second_products(c, 2 * pair, 2))
             for i, s in enumerate(slabs):
                 y_bank = psum.tile([PART, HALF], F32, name="y_bank", tag=("words", "y")[i])
                 for t in range(4):
-                    for k in range(3):
-                        nc.tensor.matmul(
-                            y_bank[:, PART * t : PART * (t + 1)],
-                            lhsT=parts[2 + t // 2][k][:, t % 2, PART * i : PART * (i + 1)], rhs=ident[:],
-                            is_transpose=True, start=(k == 0), stop=(k == 2),
-                        )
-                nc.scalar.copy(wide[s], y_bank[:])
+                    add_turned(y_bank[:, PART * t : PART * (t + 1)], parts[2 + t // 2], t % 2, i)
+                if pair == 0:
+                    subtract_own(wide[s], s, y_bank[:])
+                else:
+                    nc.scalar.copy(wide[s], y_bank[:])
                 put(page1_sb[s], idx4, HALF, HALF, wide[s], wgo_sb[:, HALF:])
                 nc.sync.dma_start(out[rows(s), :], page1_sb[s][:])

@@ -53,11 +53,6 @@ def tile_list_cork_batch_page_kernel(
         make_identity(nc, ident[:])
         tab_sc = sb.tile([PART, T], U8, name="tab_sc", tag="tab_sc", align_bytes=64)
         nc.vector.memset(tab_sc[:].bitcast(I32), 0)
-        for q in range(4):
-            nc.gpsimd.dma_start(
-                tab_sc[32 * q : 32 * q + 4 * PASSES, :].bitcast(I32),
-                tab_scales[:, 4 * q : 4 * q + 4, :].bitcast(I32),
-            )
         w2_sc = sb.tile([PART, N], U8, name="w2_sc", align_bytes=64)
         nc.vector.memset(w2_sc[:].bitcast(I32), 0)
 
@@ -72,7 +67,7 @@ def tile_list_cork_batch_page_kernel(
             raws = []
             for a in range(PASSES):
                 raw = sb.tile([PART, 4, PART], F32, name="w1_raw", tag="w1_raw", bufs=2 * PASSES)
-                (nc.scalar if s == 0 else nc.sync).dma_start(
+                nc.sync.dma_start(
                     raw[:],
                     w1[512 * a : 512 * (a + 1), PART * s : PART * (s + 1)].rearrange("(p i) c -> p i c", i=4),
                 )
@@ -93,12 +88,19 @@ def tile_list_cork_batch_page_kernel(
             return codes, scales
 
         idx = load_list(offs, "idx")
-        w1_raw = {0: load_w1(0)}
         tab_w = []
+        w1_raw = {}
         for a in range(PASSES):
             t = sb.tile([PART, T], U32, name="tab_w", tag="big%d" % a, align_bytes=64)
             nc.sync.dma_start(t[:].bitcast(I32), tab_words[a].rearrange("p t i -> p (t i)").bitcast(I32))
             tab_w.append(t)
+            if a == 0:
+                for q in range(4):
+                    nc.sync.dma_start(
+                        tab_sc[32 * q : 32 * q + 4 * PASSES, :].bitcast(I32),
+                        tab_scales[:, 4 * q : 4 * q + 4, :].bitcast(I32),
+                    )
+                w1_raw[0] = load_w1(0)
             if a == 0:
                 for i, vec in enumerate((gain, base, keep)):
                     nc.sync.dma_start(vec_rows[SLABS * i : SLABS * (i + 1), :], vec.rearrange("(s p) -> s p", p=PART))
@@ -298,7 +300,7 @@ def tile_list_cork_batch_page_kernel(
                         bank[:, jt, :], lhsT=x_codes[:, cols].bitcast(FP8X4), lhsT_scale=x_sc[:, cols],
                         rhs=w, rhs_scale=w_scale[:, outs], start=True, stop=True,
                     )
-                part = sb.tile([PART, 2, width], F32, name="part", tag="part", bufs=10)
+                part = sb.tile([PART, 2, width], F32, name="part", tag="part", bufs=12)
                 nc.scalar.activation(part[:], bank[:], func)
                 parts.append(part)
             return parts
@@ -313,13 +315,29 @@ def tile_list_cork_batch_page_kernel(
         def subtract_own(values, s, sums):
             nc.vector.scalar_tensor_tensor(values, values, minus_keep[:, s : s + 1], sums, ALU.mult, ALU.add)
 
+        def own_term(chunks, first, values):
+            for s in (first, first + 1):
+                nc.scalar.activation(values[s], values[s], ACT.Copy, scale=minus_keep[:, s : s + 1])
+            parts = {}
+            for c in chunks:
+                bank = pair_bank((c + first // 2) % 2)
+                for s in (first, first + 1):
+                    turn(bank, c, s)
+                own = sb.tile([PART, 2, 2 * PART], F32, name="part", tag="part", bufs=12)
+                nc.scalar.copy(own[:], bank[:])
+                parts[c] = [own]
+            return parts
+
         def finish(c, first, count, parts, tag):
             y_bank = psum.tile([PART, count, CHUNK], F32, name="y_bank", tag=tag)
             for i in range(count):
                 for jt in range(2):
                     add_turned(y_bank[:, i, PART * jt : PART * (jt + 1)], parts, jt, i)
-            for i in range(count):
-                subtract_own(x[c, first + i], first + i, y_bank[:, i, :])
+            if len(parts) == 3:
+                nc.scalar.copy(x_second[:, CHUNK * first : CHUNK * (first + count)], y_bank[:].rearrange("p i j -> p (i j)"))
+            else:
+                for i in range(count):
+                    subtract_own(x[c, first + i], first + i, y_bank[:, i, :])
             for s in range(first, first + count):
                 put(page1_sb[s], idx4, CHUNK * c, CHUNK, x[c, s], wgo_sb[:, CHUNK * c : CHUNK * (c + 1)])
 
@@ -333,6 +351,7 @@ def tile_list_cork_batch_page_kernel(
                 round_slabs(c, 2 * pair, 2, bank)
             quantise_x(c, tag)
 
+        x_second = limited
         for s in range(SLABS):
             fetch(CHUNK, CHUNK, s, limited[:, CHUNK * s : CHUNK * (s + 1)])
         wide = {s: fac[:, HALF * s : HALF * (s + 1)] for s in range(2)}
@@ -355,7 +374,7 @@ def tile_list_cork_batch_page_kernel(
                 rhs=x_codes[:, :CHUNK].bitcast(FP8X4), rhs_scale=x_sc[:, :CHUNK], start=True, stop=True,
             )
             sums.append(bank)
-        bounded = sb.tile([PART, CHUNK], F32, name="bounded", tag="part", bufs=10)
+        bounded = sb.tile([PART, CHUNK], F32, name="bounded", tag="part", bufs=12)
         nc.scalar.activation(bounded[:], sums[1][:], ACT.Tanh)
         subtract_own(x[0, 0], 0, sums[0][:])
         nc.vector.tensor_tensor(x[0, 0], x[0, 0], bounded[:], ALU.add)
@@ -365,7 +384,10 @@ def tile_list_cork_batch_page_kernel(
         front(1, "words")
         finish(0, 1, 1, parts[0], "words")
         finish(0, 2, 2, parts[1], "y")
-        parts = [second_products(1, 2 * pair, 2) for pair in range(2)]
+        parts = []
+        for pair in range(2):
+            own = own_term((1,), 2 * pair, {s: x[1, s] for s in range(SLABS)})[1] if pair in () else []
+            parts.append(own + second_products(1, 2 * pair, 2))
         front(2, "words")
         finish(1, 0, 2, parts[0], "words")
         front(3, "y")
@@ -373,26 +395,13 @@ def tile_list_cork_batch_page_kernel(
 
         for pair in range(2):
             slabs = (2 * pair, 2 * pair + 1)
-            parts = {2: [], 3: []}
-            if pair == 1:
-                for s in slabs:
-                    nc.scalar.activation(wide[s], wide[s], ACT.Copy, scale=minus_keep[:, s : s + 1])
-                for c in (2, 3):
-                    bank = pair_bank(c % 2)
-                    for s in slabs:
-                        turn(bank, c, s)
-                    own = sb.tile([PART, 2, 2 * PART], F32, name="part", tag="part", bufs=10)
-                    nc.scalar.copy(own[:], bank[:])
-                    parts[c].append(own)
+            parts = own_term((2, 3), 2 * pair, wide)
             for c in (2, 3):
                 parts[c].extend(second_products(c, 2 * pair, 2))
             for i, s in enumerate(slabs):
                 y_bank = psum.tile([PART, HALF], F32, name="y_bank", tag=("words", "y")[i])
                 for t in range(4):
                     add_turned(y_bank[:, PART * t : PART * (t + 1)], parts[2 + t // 2], t % 2, i)
-                if pair == 0:
-                    subtract_own(wide[s], s, y_bank[:])
-                else:
-                    nc.scalar.copy(wide[s], y_bank[:])
+                nc.scalar.copy(wide[s], y_bank[:])
                 put(page1_sb[s], idx4, HALF, HALF, wide[s], wgo_sb[:, HALF:])
                 nc.sync.dma_start(out[rows(s), :], page1_sb[s][:])

from contextlib import ExitStack

import concourse.mybir as mybir
from concourse.masks import make_identity

K, T, S, H, T2, P, N = 1536, 4096, 1024, 512, 2048, 1024, 512
FLOPS = 2 * K * H * S + 2 * 2 * H * N * P

F32 = mybir.dt.float32
BF16 = mybir.dt.bfloat16
I32 = mybir.dt.int32
U32 = mybir.dt.uint32
U16 = mybir.dt.uint16
U8 = mybir.dt.uint8
FP8X4 = mybir.dt.float8_e4m3fn_x4
FP4X4 = mybir.dt.float4_e2m1fn_x4
ALU = mybir.AluOpType
ACT = mybir.ActivationFunctionType

PART = 128
PASSES = K // 512
SLABS = H // PART
HALF = S // 2
CHUNK = 256
CHUNKS = P // CHUNK


def tile_list_cork_batch_page_kernel(
    tc, tab_words, tab_scales, offs, w1, cap, gain, page0, wgs, offs2, offs3, base,
    w2_words, w2_scales, w3, keep, page1, wgo, offs4, out,
):
    nc = tc.nc
    with ExitStack() as ctx:
        lists = ctx.enter_context(tc.tile_pool(name="lists", bufs=1))
        sb = ctx.enter_context(tc.tile_pool(name="sb", bufs=1))
        psum = ctx.enter_context(tc.psum_pool(name="psum", bufs=1))

        def load_list(src, name):
            t = lists.tile([PART, S // 16], U16, name=name)
            nc.sync.dma_start(t[:], src)
            return t

        def entries(list_tile, first, count):
            return list_tile[:, first // 16 : (first + count) // 16]

        warm = sb.tile([PART, 8], F32, name="warm")
        nc.vector.memset(warm[:, 0:1], 0.0)
        nc.scalar.activation(warm[:, 4:5], warm[:, 0:1], ACT.Tanh)

        vec_rows = sb.tile([PART, PART], F32, name="vec_rows")
        nc.gpsimd.memset(vec_rows[:], 0.0)
        ident = sb.tile([PART, PART], F32, name="ident")
        make_identity(nc, ident[:])
        tab_sc = sb.tile([PART, T], U8, name="tab_sc", tag="tab_sc", align_bytes=64)
        nc.vector.memset(tab_sc[:].bitcast(I32), 0)
        w2_sc = sb.tile([PART, N], U8, name="w2_sc", align_bytes=64)
        nc.vector.memset(w2_sc[:].bitcast(I32), 0)


        def interleave(copy, dst, src):
            copy(
                dst.rearrange("p (c k i) -> p c i k", k=4, i=4),
                src.rearrange("p i (c k) -> p c i k", k=4),
            )

        def load_w1(s):
            raws = []
            for a in range(PASSES):
                raw = sb.tile([PART, 4, PART], F32, name="w1_raw", tag="w1_raw", bufs=2 * PASSES)
                nc.sync.dma_start(
                    raw[:],
                    w1[512 * a : 512 * (a + 1), PART * s : PART * (s + 1)].rearrange("(p i) c -> p i c", i=4),
                )
                raws.append(raw)
            return raws

        def quantise_w1(s, raws):
            copy = nc.vector.tensor_copy if s == 0 else nc.scalar.copy
            codes = sb.tile([PART, PASSES * PART], U32, name="w1_codes", tag="w1_codes%d" % s, align_bytes=64)
            scales = sb.tile([PART, PASSES * PART], U8, name="w1_scales%d" % s, align_bytes=64)
            for lo, hi, tag in ((0, 2, "w1_bf%d" % s), (2, 3, "w1_bf_last")):
                grouped = sb.tile([PART, 512 * (hi - lo)], BF16, name="w1_bf", tag=tag, align_bytes=64)
                for a in range(lo, hi):
                    interleave(copy, grouped[:, 512 * (a - lo) : 512 * (a - lo + 1)], raws[a][:])
                nc.vector.quantize_mx(
                    codes[:, PART * lo : PART * hi].bitcast(FP8X4), scales[:, PART * lo : PART * hi], grouped[:]
                )
            return codes, scales

        idx = load_list(offs, "idx")
        tab_w = []
        w1_raw = {}
        for a in range(PASSES):
            t = sb.tile([PART, T], U32, name="tab_w", tag="big%d" % a, align_bytes=64)
            nc.sync.dma_start(t[:].bitcast(I32), tab_words[a].rearrange("p t i -> p (t i)").bitcast(I32))
            tab_w.append(t)
            if a == 0:
                for q in range(4):
                    nc.sync.dma_start(
                        tab_sc[32 * q : 32 * q + 4 * PASSES, :].bitcast(I32),
                        tab_scales[:, 4 * q : 4 * q + 4, :].bitcast(I32),
                    )
                w1_raw[0] = load_w1(0)
            if a == 0:
                for i, vec in enumerate((gain, base, keep)):
                    nc.sync.dma_start(vec_rows[SLABS * i : SLABS * (i + 1), :], vec.rearrange("(s p) -> s p", p=PART))
        vec_bank = psum.tile([PART, PART], F32, name="vec_bank", tag="y")
        nc.tensor.transpose(vec_bank[:], vec_rows[:], ident[:])
        vec_cols = sb.tile([PART, 2 * SLABS], F32, name="vec_cols")
        nc.scalar.copy(vec_cols[:], vec_bank[:, : 2 * SLABS])
        gain_sb, base_sb = vec_cols[:, :SLABS], vec_cols[:, SLABS:]
        minus_keep = sb.tile([PART, SLABS], F32, name="minus_keep")
        nc.scalar.activation(minus_keep[:], vec_bank[:, 2 * SLABS : 3 * SLABS], ACT.Copy, scale=-1.0)
        wgs_sb = sb.tile([PART, S], F32, name="wgs_sb")
        cap_first = [sb.tile([PART, HALF], F32, name="cap_first", tag="w1_codes%d" % (h + 1), align_bytes=64) for h in range(2)]
        cap_sb = {s: sb.tile([PART, S], F32, name="cap_sb%d" % s) for s in range(1, SLABS)}
        page0_sb = [sb.tile([PART, T2], F32, name="page0_sb%d" % s) for s in range(SLABS)]

        def rows(s):
            return slice(PART * s, PART * (s + 1))

        nc.sync.dma_start(wgs_sb[:, :HALF], wgs[:, :HALF])
        nc.sync.dma_start(cap_first[0][:], cap[rows(0), :HALF])
        idx2 = load_list(offs2, "idx2")
        nc.sync.dma_start(page0_sb[0][:], page0[rows(0), :])
        w1_raw[1] = load_w1(1)
        nc.sync.dma_start(cap_first[1][:], cap[rows(0), HALF:])
        nc.sync.dma_start(wgs_sb[:, HALF:], wgs[:, HALF:])

        w1_q = {0: quantise_w1(0, w1_raw[0])}

        v_sc = sb.tile([PART, S], U8, name="v_sc", align_bytes=64)
        nc.vector.tensor_copy(v_sc[:], tab_sc[:].indirect(idx[:]))
        v_w = []
        for a in range(PASSES):
            t = sb.tile([PART, S], U32, name="v_w%d" % a, tag="tab_sc" if a == PASSES - 1 else "v_w%d" % a, align_bytes=64)
            if a < PASSES - 1:
                nc.vector.tensor_copy(t[:], tab_w[a][:].indirect(idx[:]))
            else:
                for h in range(2):
                    nc.vector.tensor_copy(
                        t[:, HALF * h : HALF * (h + 1)], tab_w[a][:].indirect(entries(idx, HALF * h, HALF))
                    )
            v_w.append(t)

        def first_product(s, h):
            codes, scales = w1_q[s]
            bank = psum.tile([PART, HALF], F32, name="h_bank", tag="acc", bufs=4)
            cols = slice(HALF * h, HALF * (h + 1))
            for a in range(PASSES):
                nc.tensor.matmul_mx(
                    bank[:],
                    lhsT=codes[:, PART * a : PART * (a + 1)].bitcast(FP8X4),
                    lhsT_scale=scales[:, PART * a : PART * (a + 1)],
                    rhs=v_w[a][:, cols].bitcast(FP8X4),
                    rhs_scale=v_sc[4 * a : PART, cols],
                    start=(a == 0),
                    stop=(a == PASSES - 1),
                )
            return bank

        def factors(s, first, count):
            t = sb.tile([PART, count], F32, name="factor", tag="factor%d" % (s % 2 if s < SLABS - 1 else 2), bufs=1)
            nc.scalar.activation(t[:], wgs_sb[:, first : first + count], ACT.Copy, scale=gain_sb[:, s : s + 1])
            return t

        def put(page, list_tile, first, count, values, weights):
            nc.vector.tensor_tensor(
                page[:].indirect(entries(list_tile, first, count)), values, weights, ALU.mult
            )

        banks = [first_product(0, h) for h in range(2)]
        fac0 = sb.tile([PART, S], F32, name="factor", tag="factor0", bufs=1)
        nc.scalar.activation(fac0[:, :HALF], wgs_sb[:, :HALF], ACT.Copy, scale=gain_sb[:, 0:1])
        limited = sb.tile([PART, HALF], F32, name="limited", tag="limited_first")
        nc.vector.tensor_tensor(limited[:], banks[0][:], cap_first[0][:], ALU.min)
        put(page0_sb[0], idx2, 0, HALF, limited[:], fac0[:, :HALF])
        w1_q[1] = quantise_w1(1, w1_raw[1])
        nc.scalar.activation(fac0[:, HALF:], wgs_sb[:, HALF:], ACT.Copy, scale=gain_sb[:, 0:1])
        limited = sb.tile([PART, HALF], F32, name="limited", tag="w1_bf1", align_bytes=64)
        nc.vector.tensor_tensor(limited[:], banks[1][:], cap_first[1][:], ALU.min)
        put(page0_sb[0], idx2, HALF, HALF, limited[:], fac0[:, HALF:])

        nc.sync.dma_start(cap_sb[1][:], cap[rows(1), :])
        w1_raw[2] = load_w1(2)
        nc.sync.dma_start(page0_sb[1][:], page0[rows(1), :])
        idx3 = load_list(offs3, "idx3")
        nc.sync.dma_start(cap_sb[2][:], cap[rows(2), :])
        w1_raw[3] = load_w1(3)
        nc.sync.dma_start(page0_sb[2][:], page0[rows(2), :])
        w3_raw = sb.tile([PART, 4, N], F32, name="w3_raw")
        nc.sync.dma_start(w3_raw[:], w3.rearrange("(p i) n -> p i n", i=4))
        nc.sync.dma_start(cap_sb[3][:], cap[rows(3), :])
        nc.sync.dma_start(page0_sb[3][:], page0[rows(3), :])
        w2_w = sb.tile([PART, 2 * N], U8, name="w2_w", align_bytes=64)
        nc.sync.dma_start(w2_w[:].bitcast(I32), w2_words[0].bitcast(I32))
        for q in range(4):
            nc.sync.dma_start(
                w2_sc[32 * q : 32 * q + 4, :].bitcast(I32),
                w2_scales[0, 4 * q : 4 * q + 4, :].bitcast(I32),
            )
        idx4 = load_list(offs4, "idx4")
        wgo_sb = sb.tile([PART, P], F32, name="wgo_sb")
        nc.sync.dma_start(wgo_sb[:], wgo)
        page1_sb = []
        for s in range(SLABS):
            t = sb.tile([PART, T2], F32, name="page1_sb", tag="big%d" % s, align_bytes=64)
            nc.sync.dma_start(t[:], page1[rows(s), :])
            page1_sb.append(t)

        x = {}
        xt_bf = {}

        def fetch(first, count, s, dst):
            nc.vector.tensor_copy(dst, page0_sb[s][:].indirect(entries(idx3, first, count)))
            for c in range(first // CHUNK, (first + count) // CHUNK):
                x[c, s] = dst[:, CHUNK * c - first : CHUNK * (c + 1) - first]

        def add_base(values, s):
            nc.scalar.activation(values, values, ACT.Identity, bias=base_sb[:, s : s + 1])

        def turn(bank, c, s):
            for jt in range(2):
                nc.tensor.transpose(
                    bank[:, jt, PART * (s % 2) : PART * (s % 2 + 1)], x[c, s][:, PART * jt : PART * (jt + 1)], ident[:]
                )

        def pair_bank(pair):
            return psum.tile([PART, 2, 2 * PART], F32, name="xt_bank", tag="xt%d" % pair)

        def round_slabs(c, first, count, bank):
            if first == 0:
                xt_bf[c] = sb.tile([PART, 2, 2, 2 * PART], BF16, name="xt_bf", tag="xt_bf", bufs=2)
            lo = PART * (first % 2)
            nc.scalar.copy(
                xt_bf[c][:, :, :, 64 * first : 64 * (first + count)].rearrange("p t u (q e) -> p t u q e", e=2),
                bank[:, :, lo : lo + PART * count].rearrange("p t (q u e) -> p t u q e", u=2, e=2),
            )

        first_banks = [pair_bank(pair) for pair in range(2)]
        for s in range(1, SLABS):
            banks = [first_product(s, h) for h in range(2)]
            fac = factors(s, 0, S)
            if s < SLABS - 1:
                w1_q[s + 1] = quantise_w1(s + 1, w1_raw[s + 1])
                limited = sb.tile([PART, S], F32, name="limited", tag="w1_bf%d" % (s + 1), align_bytes=64)
            else:
                w3_bf = sb.tile([PART, 4 * N], BF16, name="w3_bf", tag="w3_bf", align_bytes=64)
                interleave(nc.scalar.copy, w3_bf[:], w3_raw[:])
                w3_codes = sb.tile([PART, N], U32, name="w3_codes", align_bytes=64)
                w3_sc = sb.tile([PART, N], U8, name="w3_sc", align_bytes=64)
                nc.vector.quantize_mx(w3_codes[:].bitcast(FP8X4), w3_sc[:], w3_bf[:])
                limited = sb.tile([PART, S], F32, name="limited", tag="w3_bf", align_bytes=64)
            for h in range(2):
                cols = slice(HALF * h, HALF * (h + 1))
                nc.vector.tensor_tensor(limited[:, cols], banks[h][:], cap_sb[s][:, cols], ALU.min)
            fetch(0, CHUNK, s - 1, cap_sb[s][:, :CHUNK])
            put(page0_sb[s], idx2, 0, S, limited[:], fac[:])
            add_base(x[0, s - 1], s - 1)
            turn(first_banks[(s - 1) // 2], 0, s - 1)
            if s == 2:
                round_slabs(0, 0, 2, first_banks[0])
            if s == 3:
                round_slabs(0, 2, 1, first_banks[1])
        last = SLABS - 1
        fetch(0, CHUNK, last, cap_sb[last][:, HALF : HALF + CHUNK])
        add_base(x[0, last], last)
        turn(first_banks[1], 0, last)
        round_slabs(0, last, 1, first_banks[1])

        x_codes = sb.tile([PART, P], U32, name="x_codes", align_bytes=64)
        x_sc = sb.tile([PART, P], U8, name="x_sc", align_bytes=64)

        def quantise_x(c, tag):
            words = xt_bf[c][:].rearrange("p t u r -> p (t u r)").bitcast(F32)
            bank = psum.tile([PART, 2, 2, PART], F32, name="word_bank", tag=tag)
            for jt in range(2):
                for u in range(2):
                    nc.tensor.transpose(bank[:, jt, u, :], words[:, PART * (2 * jt + u) : PART * (2 * jt + u + 1)], ident[:])
            grouped = sb.tile([PART, 4 * CHUNK], BF16, name="grouped", tag="grouped%d" % min(c, 1), bufs=1 if c == 0 else 2, align_bytes=64)
            nc.scalar.copy(
                grouped[:].bitcast(F32).rearrange("p (t j u) -> p t j u", t=2, u=2),
                bank[:].rearrange("p t u j -> p t j u"),
            )
            cols = slice(CHUNK * c, CHUNK * (c + 1))
            nc.vector.quantize_mx(x_codes[:, cols].bitcast(FP8X4), x_sc[:, cols], grouped[:])

        def second_products(c, first, count):
            width = PART * count
            outs = slice(PART * first, PART * (first + count))
            parts = []
            for w, w_scale, func in (
                (w2_w[:, 2 * outs.start : 2 * outs.stop].bitcast(FP4X4), w2_sc, ACT.Tanh),
                (w3_codes[:, outs].bitcast(FP8X4), w3_sc, ACT.Copy),
            ):
                bank = psum.tile([PART, 2, width], F32, name="p_bank", tag="acc", bufs=4)
                for jt in range(2):
                    cols = slice(CHUNK * c + PART * jt, CHUNK * c + PART * (jt + 1))
                    nc.tensor.matmul_mx(
                        bank[:, jt, :], lhsT=x_codes[:, cols].bitcast(FP8X4), lhsT_scale=x_sc[:, cols],
                        rhs=w, rhs_scale=w_scale[:, outs], start=True, stop=True,
                    )
                part = sb.tile([PART, 2, width], F32, name="part", tag="part", bufs=12)
                nc.scalar.activation(part[:], bank[:], func)
                parts.append(part)
            return parts

        def add_turned(dst, parts, jt, i):
            for k, part in enumerate(parts):
                nc.tensor.matmul(
                    dst, lhsT=part[:, jt, PART * i : PART * (i + 1)], rhs=ident[:],
                    is_transpose=True, start=(k == 0), stop=(k == len(parts) - 1),
                )

        def subtract_own(values, s, sums):
            nc.vector.scalar_tensor_tensor(values, values, minus_keep[:, s : s + 1], sums, ALU.mult, ALU.add)

        def own_term(chunks, first, values):
            for s in (first, first + 1):
                nc.scalar.activation(values[s], values[s], ACT.Copy, scale=minus_keep[:, s : s + 1])
            parts = {}
            for c in chunks:
                bank = pair_bank((c + first // 2) % 2)
                for s in (first, first + 1):
                    turn(bank, c, s)
                own = sb.tile([PART, 2, 2 * PART], F32, name="part", tag="part", bufs=12)
                nc.scalar.copy(own[:], bank[:])
                parts[c] = [own]
            return parts

        def finish(c, first, count, parts, tag):
            y_bank = psum.tile([PART, count, CHUNK], F32, name="y_bank", tag=tag)
            for i in range(count):
                for jt in range(2):
                    add_turned(y_bank[:, i, PART * jt : PART * (jt + 1)], parts, jt, i)
            if len(parts) == 3:
                nc.scalar.copy(x_second[:, CHUNK * first : CHUNK * (first + count)], y_bank[:].rearrange("p i j -> p (i j)"))
            else:
                for i in range(count):
                    subtract_own(x[c, first + i], first + i, y_bank[:, i, :])
            for s in range(first, first + count):
                put(page1_sb[s], idx4, CHUNK * c, CHUNK, x[c, s], wgo_sb[:, CHUNK * c : CHUNK * (c + 1)])

        def front(c, tag):
            for pair in range(2):
                bank = pair_bank(pair)
                for s in (2 * pair, 2 * pair + 1):
                    if c < 3:
                        add_base(x[c, s] if c == 1 else wide[s], s)
                    turn(bank, c, s)
                round_slabs(c, 2 * pair, 2, bank)
            quantise_x(c, tag)

        x_second = limited
        for s in range(SLABS):
            fetch(CHUNK, CHUNK, s, limited[:, CHUNK * s : CHUNK * (s + 1)])
        wide = {s: fac[:, HALF * s : HALF * (s + 1)] for s in range(2)}
        for s in range(2):
            fetch(HALF, HALF, s, wide[s])
        quantise_x(0, "words")
        x_late = sb.tile([PART, 2, HALF], F32, name="x_late", tag="grouped0", align_bytes=64)
        for s in range(2, SLABS):
            wide[s] = x_late[:, s - 2, :]
            fetch(HALF, HALF, s, wide[s])

        sums = []
        for w, w_scale in (
            (w3_codes[:, :PART].bitcast(FP8X4), w3_sc),
            (w2_w[:, : 2 * PART].bitcast(FP4X4), w2_sc),
        ):
            bank = psum.tile([PART, CHUNK], F32, name="p_bank", tag="acc", bufs=4)
            nc.tensor.matmul_mx(
                bank[:], lhsT=w, lhsT_scale=w_scale[:, :PART],
                rhs=x_codes[:, :CHUNK].bitcast(FP8X4), rhs_scale=x_sc[:, :CHUNK], start=True, stop=True,
            )
            sums.append(bank)
        bounded = sb.tile([PART, CHUNK], F32, name="bounded", tag="part", bufs=12)
        nc.scalar.activation(bounded[:], sums[1][:], ACT.Tanh)
        subtract_own(x[0, 0], 0, sums[0][:])
        nc.vector.tensor_tensor(x[0, 0], x[0, 0], bounded[:], ALU.add)
        put(page1_sb[0], idx4, 0, CHUNK, x[0, 0], wgo_sb[:, :CHUNK])

        parts = [second_products(0, 1, 1), second_products(0, 2, 2)]
        front(1, "words")
        finish(0, 1, 1, parts[0], "words")
        finish(0, 2, 2, parts[1], "y")
        parts = []
        for pair in range(2):
            own = own_term((1,), 2 * pair, {s: x[1, s] for s in range(SLABS)})[1] if pair in () else []
            parts.append(own + second_products(1, 2 * pair, 2))
        front(2, "words")
        finish(1, 0, 2, parts[0], "words")
        front(3, "y")
        finish(1, 2, 2, parts[1], "y")

        for pair in range(2):
            slabs = (2 * pair, 2 * pair + 1)
            parts = own_term((2, 3), 2 * pair, wide)
            for c in (2, 3):
                parts[c].extend(second_products(c, 2 * pair, 2))
            for i, s in enumerate(slabs):
                y_bank = psum.tile([PART, HALF], F32, name="y_bank", tag=("words", "y")[i])
                for t in range(4):
                    add_turned(y_bank[:, PART * t : PART * (t + 1)], parts[2 + t // 2], t % 2, i)
                nc.scalar.copy(wide[s], y_bank[:])
                put(page1_sb[s], idx4, HALF, HALF, wide[s], wgo_sb[:, HALF:])
                nc.sync.dma_start(out[rows(s), :], page1_sb[s][:])
